import numpy as np
import ml_dtypes


def mxq(x, axis, fmt="e4m3"):
    dtype, down = {"e4m3": (ml_dtypes.float8_e4m3fn, 7), "e5m2": (ml_dtypes.float8_e5m2, 14)}[fmt]
    v = np.moveaxis(np.asarray(x, np.float32).astype(ml_dtypes.bfloat16).astype(np.float64), axis, -1)
    blocks = v.reshape(v.shape[:-1] + (-1, 32))
    amax = np.abs(blocks).max(-1, keepdims=True)
    byte = np.maximum(np.where(amax > 0, np.frexp(amax)[1] - 1 + 127, 0) - down, 1)
    scale = np.exp2(byte - 127.0)
    codes = (blocks / scale).astype(np.float32).astype(dtype).astype(np.float64)
    return np.moveaxis((codes * scale).reshape(v.shape), -1, axis)


WIDE = False


def mx_kscale(k):
    if not WIDE:
        return np.ones(k)
    levels = np.array([10, -10, 5, -5, 0])
    if k % 512:
        return np.exp2(np.random.permutation(np.resize(levels, k // 32))).repeat(32)
    a = np.empty((k // 512, 16))
    for p in range(k // 512):
        a[p, :8] = np.random.permutation(np.resize(levels, 8))
        for g in range(8):
            far = levels[np.abs(levels - a[p, g]) >= 10]
            a[p, g + 8] = far[np.random.randint(len(far))]
    return np.exp2(a.ravel()).repeat(32)


def f64(x):
    return np.asarray(x).astype(np.float64)


def striped8(idx):
    return np.asarray(idx).reshape(8, -1, 16).transpose(0, 2, 1).reshape(128, -1).astype(np.uint16)


def unstriped8(offs):
    return offs.reshape(8, 16, -1).transpose(0, 2, 1).reshape(8, -1).astype(np.int64)


def pick8(x, idx, run):
    r = np.arange(len(x))
    return x[r[:, None], idx[r % (8 * run) // run]]


E2M1 = np.array([0.0, 0.5, 1.0, 1.5, 2.0, 3.0, 4.0, 6.0, -0.0, -0.5, -1.0, -1.5, -2.0, -3.0, -4.0, -6.0])


def pack_weight(w, fmt):
    k, n = w.shape
    w = f64(np.asarray(w, np.float32).astype(ml_dtypes.bfloat16)).reshape(k // 32, 32, n)
    amax = np.abs(w).max(1)
    if fmt == "e4m3":
        byte = np.frexp(amax)[1] - 1 + 127 - 7
    else:
        mant, ex = np.frexp(amax / 6.0)
        byte = np.where(mant > 0.5, ex, ex - 1) + 127
    byte = np.clip(np.where(amax > 0, byte, 1), 1, 254)
    scaled = (w * np.exp2(127.0 - byte)[:, None, :]).reshape(k, n).astype(np.float32)
    by_word = np.ascontiguousarray(scaled.reshape(k // 512, 128, 4, n).transpose(0, 1, 3, 2))
    if fmt == "e4m3":
        words = by_word.astype(ml_dtypes.float8_e4m3fn).view(np.uint8)
    else:
        c = by_word.astype(ml_dtypes.float4_e2m1fn).view(np.uint8) & 0xF
        words = (c[..., 0::2] | (c[..., 1::2] << 4)).reshape(k // 512, 128, 2 * n)
    return np.ascontiguousarray(words), np.ascontiguousarray(byte.astype(np.uint8).reshape(k // 512, 16, n))


def unpack_weight(words, scales, fmt):
    g, _, n = scales.shape
    words = np.ascontiguousarray(words).reshape(g, 128, n, -1)
    if fmt == "e4m3":
        vals = words.view(ml_dtypes.float8_e4m3fn).astype(np.float64)
    else:
        nib = np.empty((g, 128, n, 4), np.uint8)
        nib[..., 0::2] = words & 0xF
        nib[..., 1::2] = words >> 4
        vals = E2M1[nib]
    vals = vals * np.repeat(np.exp2(scales.astype(np.float64) - 127.0), 8, axis=1)[..., None]
    return vals.transpose(0, 1, 3, 2).reshape(g * 512, n)


D, T, I, Q = 512, 1024, 512, 128


def setup_inputs():
    n = np.random.standard_normal
    idx = np.stack([np.random.permutation(T)[:I] for _ in range(8)])
    idx2 = np.stack([np.random.permutation(T)[:I] for _ in range(8)])
    idx3 = np.stack([np.random.permutation(T)[:I] for _ in range(8)])
    fd = mx_kscale(D)
    keysp = pack_weight(n((D, T)) / fd[:, None], "e4m3")
    return {
        "query": (n((D, Q)) * 0.9 / np.sqrt(D) * fd[:, None]).astype(np.float32),
        "query2": (n((D, Q)) * 0.9 / np.sqrt(D) * fd[:, None]).astype(np.float32),
        "keys_words": keysp[0],
        "keys_scales": keysp[1],
        "lam": (np.random.uniform(0.5, 1.3, (Q, 1))).astype(np.float32),
        "width": (np.random.uniform(0.3, 0.8, (Q, 1))).astype(np.float32),
        "old": (1.0 * n((Q, T))).astype(np.float32),
        "offs": striped8(idx),
        "offs2": striped8(idx2),
        "offs3": striped8(idx3),
    }


def reference(query, query2, keys_words, keys_scales, lam, width, old, offs, offs2, offs3):
    idx = unstriped8(offs)
    idx2 = unstriped8(offs2)
    idx3 = unstriped8(offs3)
    keysu = unpack_weight(keys_words, keys_scales, "e4m3")
    queryq = mxq(f64(query), 0, "e4m3")
    a = queryq.T @ keysu
    query2q = mxq(f64(query2), 0, "e4m3")
    b = query2q.T @ keysu
    s = (np.maximum(pick8(a, idx, 16), pick8(b, idx2, 16)) - np.maximum(pick8(a, idx2, 16), pick8(b, idx, 16))) * f64(lam)
    ce = (s - np.mean(s, axis=1, keepdims=True)) / f64(width)
    p = 1.0 / (np.square(ce) + 1.0)
    w = p / np.sum(p, axis=1, keepdims=True)
    ws = w * 512.0
    f1 = np.zeros((Q, T))
    f1[np.arange(Q)[:, None], idx[np.arange(Q) % 128 // 16]] = ws
    f2 = f1 + f64(old)
    y = pick8(f2, idx3, 16)
    return y

@@ -1,0 +1,204 @@
+from contextlib import ExitStack
+
+import concourse.mybir as mybir
+
+D, T, I, Q = 512, 1024, 512, 128
+FLOPS = 2 * 2 * D * T * Q
+
+F32 = mybir.dt.float32
+BF16 = mybir.dt.bfloat16
+I32 = mybir.dt.int32
+U32 = mybir.dt.uint32
+U16 = mybir.dt.uint16
+U8 = mybir.dt.uint8
+FP8X4 = mybir.dt.float8_e4m3fn_x4
+ALU = mybir.AluOpType
+ACT = mybir.ActivationFunctionType
+
+P = 128
+PACK = 4
+BANK = 512
+HALF = I // 2
+LIST_COLS = I // 16
+PIECE = 256
+VECTOR_SHARE = 352
+
+
+def tile_attend_exchanged_typical_through_heads_kernel(
+    tc, query, query2, keys_words, keys_scales, lam, width, old, offs, offs2, offs3, out
+):
+    nc = tc.nc
+    with ExitStack() as ctx:
+        pool = ctx.enter_context(tc.tile_pool(name="pool", bufs=1))
+        psum = ctx.enter_context(tc.psum_pool(name="psum", bufs=1))
+
+        def sb(name, shape, dtype):
+            return pool.tile(shape, dtype, name=name, align_bytes=64)
+
+        list1 = pool.tile([P, LIST_COLS], U16, name="list1")
+        list2 = pool.tile([P, LIST_COLS], U16, name="list2")
+        list3 = pool.tile([P, LIST_COLS], U16, name="list3")
+
+        key_scales = sb("key_scales", [P, T], U8)
+        nc.vector.memset(key_scales[:].bitcast(I32), 0)
+        f1 = sb("f1", [P, T], F32)
+
+        words = keys_words[0].rearrange("p n t -> p (n t)")
+        raw = [sb("raw%d" % j, [P, PACK, Q], F32) for j in range(2)]
+        key_codes = [sb("key_codes%d" % c, [P, BANK], U32) for c in range(2)]
+        width_sb = sb("width_sb", [P, 1], F32)
+        lam_sb = sb("lam_sb", [P, 1], F32)
+        old_sb = sb("old_sb", [P, T], F32)
+
+        def load_query(j, src):
+            nc.sync.dma_start(out=raw[j][:], in_=src.rearrange("(p j) w -> p j w", j=PACK))
+
+        def load_keys(c):
+            nc.sync.dma_start(
+                out=key_codes[c][:].bitcast(I32),
+                in_=words[:, c * BANK * PACK : (c + 1) * BANK * PACK].bitcast(I32),
+            )
+
+        load_query(0, query)
+        for r in range(4):
+            nc.scalar.dma_start(
+                out=key_scales[r:P:32, :].bitcast(I32), in_=keys_scales[0, r:16:4, :].bitcast(I32)
+            )
+        load_keys(0)
+        load_query(1, query2)
+        load_keys(1)
+        nc.gpsimd.dma_start(out=width_sb[:], in_=width)
+        nc.gpsimd.dma_start(out=lam_sb[:], in_=lam)
+        nc.vector.memset(f1[:], 0.0)
+        nc.sync.dma_start(list1[:], offs)
+        nc.sync.dma_start(list2[:], offs2)
+        nc.sync.dma_start(list3[:], offs3)
+        nc.sync.dma_start(out=old_sb[:], in_=old)
+
+        q_codes = []
+        q_scales = []
+        for j in range(2):
+            grouped = sb("grouped%d" % j, [P, Q, PACK], BF16)
+            nc.vector.tensor_copy(
+                out=grouped[:].rearrange("p (c i) t -> p c t i", i=4),
+                in_=raw[j][:].rearrange("p t (c i) -> p c t i", i=4),
+            )
+            codes = sb("q_codes%d" % j, [P, Q], U32)
+            scales = sb("q_scales%d" % j, [P, Q], U8)
+            nc.vector.quantize_mx(
+                out=codes[:].bitcast(FP8X4),
+                scales=scales[:],
+                in_=grouped[:].rearrange("p w t -> p (w t)"),
+            )
+            q_codes.append(codes)
+            q_scales.append(scales)
+
+        root = sb("root", [P, 1], F32)
+        nc.scalar.activation(out=root[:], in_=width_sb[:], func=ACT.Abs_reciprocal_sqrt)
+        ratio = sb("ratio", [P, 1], F32)
+        nc.gpsimd.tensor_scalar(
+            out=ratio[:], in0=root[:], scalar1=root[:], scalar2=lam_sb[:], op0=ALU.mult, op1=ALU.mult
+        )
+        slope = sb("slope", [P, 1], F32)
+        nc.gpsimd.tensor_scalar(
+            out=slope[:], in0=ratio[:], scalar1=ratio[:], scalar2=1.0 / (I * I), op0=ALU.mult, op1=ALU.mult
+        )
+
+        scores = [sb("a", [P, T], F32), sb("b", [P, T], F32)]
+        for j in range(2):
+            for n in range(T // PIECE):
+                c, lo = divmod(n * PIECE, BANK)
+                cols = slice(n * PIECE, (n + 1) * PIECE)
+                acc = psum.tile([P, PIECE], F32, name="acc%d%d" % (j, n))
+                nc.tensor.matmul_mx(
+                    out=acc[:],
+                    lhsT=q_codes[j][:].bitcast(FP8X4),
+                    lhsT_scale=q_scales[j][:],
+                    rhs=key_codes[c][:, lo : lo + PIECE].bitcast(FP8X4),
+                    rhs_scale=key_scales[:, cols],
+                    start=True,
+                    stop=True,
+                )
+                if j == 0 and n % 2 == 1:
+                    nc.vector.tensor_copy(out=scores[j][:, cols], in_=acc[:])
+                else:
+                    nc.scalar.copy(out=scores[j][:, cols], in_=acc[:])
+        a, b = scores
+
+        halves = [slice(h * HALF, (h + 1) * HALF) for h in range(2)]
+        list_halves = [slice(h * LIST_COLS // 2, (h + 1) * LIST_COLS // 2) for h in range(2)]
+
+        a1 = sb("a1", [P, I], F32)
+        a2 = sb("a2", [P, I], F32)
+        nc.vector.tensor_copy(a1[:], a[:].indirect(list1[:]))
+        nc.vector.tensor_copy(a2[:], a[:].indirect(list2[:]))
+        b2 = sb("b2", [P, I], F32)
+        b1 = [sb("b1_%d" % h, [P, HALF], F32) for h in range(2)]
+        nc.scalar.activation(b2[:], b[:].indirect(list2[:]), ACT.Copy)
+        for h in range(2):
+            nc.scalar.activation(b1[h][:], b[:].indirect(list1[:, list_halves[h]]), ACT.Copy)
+
+        m1 = sb("m1", [P, I], F32)
+        m2 = [sb("m2_%d" % h, [P, HALF], F32) for h in range(2)]
+        diff = [sb("diff_%d" % h, [P, HALF], F32) for h in range(2)]
+        sum_m1 = sb("sum_m1", [P, 1], F32)
+        sum_m2 = [sb("sum_m2_%d" % h, [P, 1], F32) for h in range(2)]
+        neg_sum = sb("neg_sum", [P, 1], F32)
+
+        nc.vector.scalar_tensor_tensor(
+            out=m1[:], in0=a1[:], scalar=1.0, in1=b2[:],
+            op0=ALU.mult, op1=ALU.max, accum_out=sum_m1[:],
+        )
+        for h in range(2):
+            nc.vector.scalar_tensor_tensor(
+                out=m2[h][:], in0=a2[:, halves[h]], scalar=1.0, in1=b1[h][:],
+                op0=ALU.mult, op1=ALU.max, accum_out=sum_m2[h][:],
+            )
+        nc.vector.tensor_tensor(out=diff[0][:], in0=m1[:, halves[0]], in1=m2[0][:], op=ALU.subtract)
+        nc.vector.scalar_tensor_tensor(
+            out=neg_sum[:], in0=sum_m2[1][:], scalar=sum_m2[0][:], in1=sum_m1[:],
+            op0=ALU.add, op1=ALU.subtract,
+        )
+        nc.vector.tensor_tensor(out=diff[1][:], in0=m1[:, halves[1]], in1=m2[1][:], op=ALU.subtract)
+
+        square = [sb("square_%d" % h, [P, HALF], F32) for h in range(2)]
+        root_p = sb("root_p", [P, I], F32)
+        for h in range(2):
+            nc.scalar.activation(out=square[h][:], in_=diff[h][:], func=ACT.Square, scale=float(I), bias=neg_sum[:])
+        for h in range(2):
+            nc.scalar.activation(
+                out=root_p[:, halves[h]], in_=square[h][:], func=ACT.Abs_reciprocal_sqrt,
+                scale=slope[:], bias=1.0,
+            )
+        part = [sb("part_%d" % h, [P, HALF], F32) for h in range(2)]
+        mean_p = [sb("mean_p%d" % h, [P, 1], F32) for h in range(2)]
+        nc.vector.scalar_tensor_tensor(
+            out=part[0][:], in0=root_p[:, halves[0]], scalar=1.0 / I, in1=root_p[:, halves[0]],
+            op0=ALU.mult, op1=ALU.mult, accum_out=mean_p[0][:],
+        )
+        nc.scalar.activation(
+            out=part[1][:], in_=root_p[:, halves[1]], func=ACT.Square, scale=I ** -0.5,
+            accum_out=mean_p[1][:],
+        )
+        root_norm = sb("root_norm", [P, 1], F32)
+        nc.scalar.activation(
+            out=root_norm[:], in_=mean_p[1][:], func=ACT.Abs_reciprocal_sqrt, bias=mean_p[0][:]
+        )
+        root_ws = sb("root_ws", [P, I], F32)
+        nc.scalar.activation(
+            out=root_ws[:, VECTOR_SHARE:], in_=root_p[:, VECTOR_SHARE:], func=ACT.Copy, scale=root_norm[:]
+        )
+        nc.vector.tensor_scalar(
+            out=root_ws[:, :VECTOR_SHARE], in0=root_p[:, :VECTOR_SHARE], scalar1=root_norm[:], scalar2=None,
+            op0=ALU.mult,
+        )
+        nc.vector.tensor_tensor(f1[:].indirect(list1[:]), root_ws[:], root_ws[:], ALU.mult)
+
+        f2 = sb("f2", [P, T], F32)
+        nc.vector.tensor_tensor(out=f2[:], in0=f1[:], in1=old_sb[:], op=ALU.add)
+
+        y = [sb("y_%d" % h, [P, HALF], F32) for h in range(2)]
+        nc.vector.tensor_copy(y[0][:], f2[:].indirect(list3[:, list_halves[0]]))
+        nc.scalar.activation(y[1][:], f2[:].indirect(list3[:, list_halves[1]]), ACT.Copy)
+        nc.sync.dma_start(out=out[:, halves[0]], in_=y[0][:])
+        nc.scalar.dma_start(out=out[:, halves[1]], in_=y[1][:])

@@ -40,7 +40,6 @@ def tile_attend_exchanged_typical_through_heads_kernel(
         list3 = pool.tile([P, LIST_COLS], U16, name="list3")
 
         key_scales = sb("key_scales", [P, T], U8)
-        nc.vector.memset(key_scales[:].bitcast(I32), 0)
         f1 = sb("f1", [P, T], F32)
 
         words = keys_words[0].rearrange("p n t -> p (n t)")
@@ -59,19 +58,19 @@ def tile_attend_exchanged_typical_through_heads_kernel(
                 in_=words[:, c * BANK * PACK : (c + 1) * BANK * PACK].bitcast(I32),
             )
 
+        nc.scalar.dma_start(out=width_sb[:], in_=width)
         load_query(0, query)
         for r in range(4):
-            nc.scalar.dma_start(
+            nc.sync.dma_start(
                 out=key_scales[r:P:32, :].bitcast(I32), in_=keys_scales[0, r:16:4, :].bitcast(I32)
             )
-        load_keys(0)
         load_query(1, query2)
+        load_keys(0)
         load_keys(1)
-        nc.gpsimd.dma_start(out=width_sb[:], in_=width)
-        nc.gpsimd.dma_start(out=lam_sb[:], in_=lam)
         nc.vector.memset(f1[:], 0.0)
         nc.sync.dma_start(list1[:], offs)
         nc.sync.dma_start(list2[:], offs2)
+        nc.sync.dma_start(out=lam_sb[:], in_=lam)
         nc.sync.dma_start(list3[:], offs3)
         nc.sync.dma_start(out=old_sb[:], in_=old)
 
@@ -94,15 +93,11 @@ def tile_attend_exchanged_typical_through_heads_kernel(
             q_scales.append(scales)
 
         root = sb("root", [P, 1], F32)
-        nc.scalar.activation(out=root[:], in_=width_sb[:], func=ACT.Abs_reciprocal_sqrt)
-        ratio = sb("ratio", [P, 1], F32)
-        nc.gpsimd.tensor_scalar(
-            out=ratio[:], in0=root[:], scalar1=root[:], scalar2=lam_sb[:], op0=ALU.mult, op1=ALU.mult
-        )
+        nc.scalar.activation(out=root[:], in_=width_sb[:], func=ACT.Abs_reciprocal_sqrt, scale=float(I))
+        inverse = sb("inverse", [P, 1], F32)
+        nc.scalar.activation(out=inverse[:], in_=root[:], func=ACT.Square)
         slope = sb("slope", [P, 1], F32)
-        nc.gpsimd.tensor_scalar(
-            out=slope[:], in0=ratio[:], scalar1=ratio[:], scalar2=1.0 / (I * I), op0=ALU.mult, op1=ALU.mult
-        )
+        nc.scalar.activation(out=slope[:], in_=inverse[:], func=ACT.Square, scale=lam_sb[:])
 
         scores = [sb("a", [P, T], F32), sb("b", [P, T], F32)]
         for j in range(2):

@@ -58,12 +58,16 @@ def tile_attend_exchanged_typical_through_heads_kernel(
                 in_=words[:, c * BANK * PACK : (c + 1) * BANK * PACK].bitcast(I32),
             )
 
-        nc.scalar.dma_start(out=width_sb[:], in_=width)
-        load_query(0, query)
-        for r in range(4):
-            nc.sync.dma_start(
+        def load_scales(queue, r):
+            queue.dma_start(
                 out=key_scales[r:P:32, :].bitcast(I32), in_=keys_scales[0, r:16:4, :].bitcast(I32)
             )
+
+        load_scales(nc.scalar, 0)
+        load_query(0, query)
+        nc.scalar.dma_start(out=width_sb[:], in_=width)
+        for r in range(1, 4):
+            load_scales(nc.sync, r)
         load_query(1, query2)
         load_keys(0)
         load_keys(1)

@@ -21,7 +21,7 @@ BANK = 512
 HALF = I // 2
 LIST_COLS = I // 16
 PIECE = 256
-VECTOR_SHARE = 352
+VECTOR_SHARE = 288
 
 
 def tile_attend_exchanged_typical_through_heads_kernel(
@@ -63,15 +63,15 @@ def tile_attend_exchanged_typical_through_heads_kernel(
                 out=key_scales[r:P:32, :].bitcast(I32), in_=keys_scales[0, r:16:4, :].bitcast(I32)
             )
 
+        nc.gpsimd.dma_start(out=width_sb[:], in_=width)
         load_scales(nc.scalar, 0)
         load_query(0, query)
-        nc.scalar.dma_start(out=width_sb[:], in_=width)
         for r in range(1, 4):
             load_scales(nc.sync, r)
         load_query(1, query2)
         load_keys(0)
         load_keys(1)
-        nc.vector.memset(f1[:], 0.0)
+        nc.gpsimd.memset(f1[:], 0.0)
         nc.sync.dma_start(list1[:], offs)
         nc.sync.dma_start(list2[:], offs2)
         nc.sync.dma_start(out=lam_sb[:], in_=lam)
@@ -118,7 +118,7 @@ def tile_attend_exchanged_typical_through_heads_kernel(
                     start=True,
                     stop=True,
                 )
-                if j == 0 and n % 2 == 1:
+                if j == 0 and n % 2 == 0:
                     nc.vector.tensor_copy(out=scores[j][:, cols], in_=acc[:])
                 else:
                     nc.scalar.copy(out=scores[j][:, cols], in_=acc[:])

from contextlib import ExitStack

import concourse.mybir as mybir

D, T, I, Q = 512, 1024, 512, 128
FLOPS = 2 * 2 * D * T * Q

F32 = mybir.dt.float32
BF16 = mybir.dt.bfloat16
I32 = mybir.dt.int32
U32 = mybir.dt.uint32
U16 = mybir.dt.uint16
U8 = mybir.dt.uint8
FP8X4 = mybir.dt.float8_e4m3fn_x4
ALU = mybir.AluOpType
ACT = mybir.ActivationFunctionType

P = 128
PACK = 4
BANK = 512
HALF = I // 2
LIST_COLS = I // 16
PIECE = 256
VECTOR_SHARE = 288


def tile_attend_exchanged_typical_through_heads_kernel(
    tc, query, query2, keys_words, keys_scales, lam, width, old, offs, offs2, offs3, out
):
    nc = tc.nc
    with ExitStack() as ctx:
        pool = ctx.enter_context(tc.tile_pool(name="pool", bufs=1))
        psum = ctx.enter_context(tc.psum_pool(name="psum", bufs=1))

        def sb(name, shape, dtype):
            return pool.tile(shape, dtype, name=name, align_bytes=64)

        list1 = pool.tile([P, LIST_COLS], U16, name="list1")
        list2 = pool.tile([P, LIST_COLS], U16, name="list2")
        list3 = pool.tile([P, LIST_COLS], U16, name="list3")

        key_scales = sb("key_scales", [P, T], U8)
        f1 = sb("f1", [P, T], F32)

        words = keys_words[0].rearrange("p n t -> p (n t)")
        raw = [sb("raw%d" % j, [P, PACK, Q], F32) for j in range(2)]
        key_codes = [sb("key_codes%d" % c, [P, BANK], U32) for c in range(2)]
        width_sb = sb("width_sb", [P, 1], F32)
        lam_sb = sb("lam_sb", [P, 1], F32)
        old_sb = sb("old_sb", [P, T], F32)

        def load_query(j, src):
            nc.sync.dma_start(out=raw[j][:], in_=src.rearrange("(p j) w -> p j w", j=PACK))

        def load_keys(c):
            nc.sync.dma_start(
                out=key_codes[c][:].bitcast(I32),
                in_=words[:, c * BANK * PACK : (c + 1) * BANK * PACK].bitcast(I32),
            )

        def load_scales(queue, r):
            queue.dma_start(
                out=key_scales[r:P:32, :].bitcast(I32), in_=keys_scales[0, r:16:4, :].bitcast(I32)
            )

        nc.gpsimd.dma_start(out=width_sb[:], in_=width)
        load_scales(nc.scalar, 0)
        load_query(0, query)
        for r in range(1, 4):
            load_scales(nc.sync, r)
        load_query(1, query2)
        load_keys(0)
        load_keys(1)
        nc.gpsimd.memset(f1[:], 0.0)
        nc.sync.dma_start(list1[:], offs)
        nc.sync.dma_start(list2[:], offs2)
        nc.sync.dma_start(out=lam_sb[:], in_=lam)
        nc.sync.dma_start(list3[:], offs3)
        nc.sync.dma_start(out=old_sb[:], in_=old)

        q_codes = []
        q_scales = []
        for j in range(2):
            grouped = sb("grouped%d" % j, [P, Q, PACK], BF16)
            nc.vector.tensor_copy(
                out=grouped[:].rearrange("p (c i) t -> p c t i", i=4),
                in_=raw[j][:].rearrange("p t (c i) -> p c t i", i=4),
            )
            codes = sb("q_codes%d" % j, [P, Q], U32)
            scales = sb("q_scales%d" % j, [P, Q], U8)
            nc.vector.quantize_mx(
                out=codes[:].bitcast(FP8X4),
                scales=scales[:],
                in_=grouped[:].rearrange("p w t -> p (w t)"),
            )
            q_codes.append(codes)
            q_scales.append(scales)

        root = sb("root", [P, 1], F32)
        nc.scalar.activation(out=root[:], in_=width_sb[:], func=ACT.Abs_reciprocal_sqrt, scale=float(I))
        inverse = sb("inverse", [P, 1], F32)
        nc.scalar.activation(out=inverse[:], in_=root[:], func=ACT.Square)
        slope = sb("slope", [P, 1], F32)
        nc.scalar.activation(out=slope[:], in_=inverse[:], func=ACT.Square, scale=lam_sb[:])

        scores = [sb("a", [P, T], F32), sb("b", [P, T], F32)]
        for j in range(2):
            for n in range(T // PIECE):
                c, lo = divmod(n * PIECE, BANK)
                cols = slice(n * PIECE, (n + 1) * PIECE)
                acc = psum.tile([P, PIECE], F32, name="acc%d%d" % (j, n))
                nc.tensor.matmul_mx(
                    out=acc[:],
                    lhsT=q_codes[j][:].bitcast(FP8X4),
                    lhsT_scale=q_scales[j][:],
                    rhs=key_codes[c][:, lo : lo + PIECE].bitcast(FP8X4),
                    rhs_scale=key_scales[:, cols],
                    start=True,
                    stop=True,
                )
                if j == 0 and n % 2 == 0:
                    nc.vector.tensor_copy(out=scores[j][:, cols], in_=acc[:])
                else:
                    nc.scalar.copy(out=scores[j][:, cols], in_=acc[:])
        a, b = scores

        halves = [slice(h * HALF, (h + 1) * HALF) for h in range(2)]
        list_halves = [slice(h * LIST_COLS // 2, (h + 1) * LIST_COLS // 2) for h in range(2)]

        a1 = sb("a1", [P, I], F32)
        a2 = sb("a2", [P, I], F32)
        nc.vector.tensor_copy(a1[:], a[:].indirect(list1[:]))
        nc.vector.tensor_copy(a2[:], a[:].indirect(list2[:]))
        b2 = sb("b2", [P, I], F32)
        b1 = [sb("b1_%d" % h, [P, HALF], F32) for h in range(2)]
        nc.scalar.activation(b2[:], b[:].indirect(list2[:]), ACT.Copy)
        for h in range(2):
            nc.scalar.activation(b1[h][:], b[:].indirect(list1[:, list_halves[h]]), ACT.Copy)

        m1 = sb("m1", [P, I], F32)
        m2 = [sb("m2_%d" % h, [P, HALF], F32) for h in range(2)]
        diff = [sb("diff_%d" % h, [P, HALF], F32) for h in range(2)]
        sum_m1 = sb("sum_m1", [P, 1], F32)
        sum_m2 = [sb("sum_m2_%d" % h, [P, 1], F32) for h in range(2)]
        neg_sum = sb("neg_sum", [P, 1], F32)

        nc.vector.scalar_tensor_tensor(
            out=m1[:], in0=a1[:], scalar=1.0, in1=b2[:],
            op0=ALU.mult, op1=ALU.max, accum_out=sum_m1[:],
        )
        for h in range(2):
            nc.vector.scalar_tensor_tensor(
                out=m2[h][:], in0=a2[:, halves[h]], scalar=1.0, in1=b1[h][:],
                op0=ALU.mult, op1=ALU.max, accum_out=sum_m2[h][:],
            )
        nc.vector.tensor_tensor(out=diff[0][:], in0=m1[:, halves[0]], in1=m2[0][:], op=ALU.subtract)
        nc.vector.scalar_tensor_tensor(
            out=neg_sum[:], in0=sum_m2[1][:], scalar=sum_m2[0][:], in1=sum_m1[:],
            op0=ALU.add, op1=ALU.subtract,
        )
        nc.vector.tensor_tensor(out=diff[1][:], in0=m1[:, halves[1]], in1=m2[1][:], op=ALU.subtract)

        square = [sb("square_%d" % h, [P, HALF], F32) for h in range(2)]
        root_p = sb("root_p", [P, I], F32)
        for h in range(2):
            nc.scalar.activation(out=square[h][:], in_=diff[h][:], func=ACT.Square, scale=float(I), bias=neg_sum[:])
        for h in range(2):
            nc.scalar.activation(
                out=root_p[:, halves[h]], in_=square[h][:], func=ACT.Abs_reciprocal_sqrt,
                scale=slope[:], bias=1.0,
            )
        part = [sb("part_%d" % h, [P, HALF], F32) for h in range(2)]
        mean_p = [sb("mean_p%d" % h, [P, 1], F32) for h in range(2)]
        nc.vector.scalar_tensor_tensor(
            out=part[0][:], in0=root_p[:, halves[0]], scalar=1.0 / I, in1=root_p[:, halves[0]],
            op0=ALU.mult, op1=ALU.mult, accum_out=mean_p[0][:],
        )
        nc.scalar.activation(
            out=part[1][:], in_=root_p[:, halves[1]], func=ACT.Square, scale=I ** -0.5,
            accum_out=mean_p[1][:],
        )
        root_norm = sb("root_norm", [P, 1], F32)
        nc.scalar.activation(
            out=root_norm[:], in_=mean_p[1][:], func=ACT.Abs_reciprocal_sqrt, bias=mean_p[0][:]
        )
        root_ws = sb("root_ws", [P, I], F32)
        nc.scalar.activation(
            out=root_ws[:, VECTOR_SHARE:], in_=root_p[:, VECTOR_SHARE:], func=ACT.Copy, scale=root_norm[:]
        )
        nc.vector.tensor_scalar(
            out=root_ws[:, :VECTOR_SHARE], in0=root_p[:, :VECTOR_SHARE], scalar1=root_norm[:], scalar2=None,
            op0=ALU.mult,
        )
        nc.vector.tensor_tensor(f1[:].indirect(list1[:]), root_ws[:], root_ws[:], ALU.mult)

        f2 = sb("f2", [P, T], F32)
        nc.vector.tensor_tensor(out=f2[:], in0=f1[:], in1=old_sb[:], op=ALU.add)

        y = [sb("y_%d" % h, [P, HALF], F32) for h in range(2)]
        nc.vector.tensor_copy(y[0][:], f2[:].indirect(list3[:, list_halves[0]]))
        nc.scalar.activation(y[1][:], f2[:].indirect(list3[:, list_halves[1]]), ACT.Copy)
        nc.sync.dma_start(out=out[:, halves[0]], in_=y[0][:])
        nc.scalar.dma_start(out=out[:, halves[1]], in_=y[1][:])
